import numpy as np
import ml_dtypes


def mxq(x, axis, fmt="e4m3"):
    dtype, down = {"e4m3": (ml_dtypes.float8_e4m3fn, 7), "e5m2": (ml_dtypes.float8_e5m2, 14)}[fmt]
    v = np.moveaxis(np.asarray(x, np.float32).astype(ml_dtypes.bfloat16).astype(np.float64), axis, -1)
    blocks = v.reshape(v.shape[:-1] + (-1, 32))
    amax = np.abs(blocks).max(-1, keepdims=True)
    byte = np.maximum(np.where(amax > 0, np.frexp(amax)[1] - 1 + 127, 0) - down, 1)
    scale = np.exp2(byte - 127.0)
    codes = (blocks / scale).astype(np.float32).astype(dtype).astype(np.float64)
    return np.moveaxis((codes * scale).reshape(v.shape), -1, axis)


WIDE = False


def mx_kscale(k):
    if not WIDE:
        return np.ones(k)
    levels = np.array([10, -10, 5, -5, 0])
    if k % 512:
        return np.exp2(np.random.permutation(np.resize(levels, k // 32))).repeat(32)
    a = np.empty((k // 512, 16))
    for p in range(k // 512):
        a[p, :8] = np.random.permutation(np.resize(levels, 8))
        for g in range(8):
            far = levels[np.abs(levels - a[p, g]) >= 10]
            a[p, g + 8] = far[np.random.randint(len(far))]
    return np.exp2(a.ravel()).repeat(32)


def f64(x):
    return np.asarray(x).astype(np.float64)


def striped(idx):
    return np.tile(idx.reshape(-1, 16).T, (8, 1)).astype(np.uint16)


def unstriped(offs):
    return offs[:16].T.reshape(-1).astype(np.int64)


E2M1 = np.array([0.0, 0.5, 1.0, 1.5, 2.0, 3.0, 4.0, 6.0, -0.0, -0.5, -1.0, -1.5, -2.0, -3.0, -4.0, -6.0])


def pack_weight(w, fmt):
    k, n = w.shape
    w = f64(np.asarray(w, np.float32).astype(ml_dtypes.bfloat16)).reshape(k // 32, 32, n)
    amax = np.abs(w).max(1)
    if fmt == "e4m3":
        byte = np.frexp(amax)[1] - 1 + 127 - 7
    else:
        mant, ex = np.frexp(amax / 6.0)
        byte = np.where(mant > 0.5, ex, ex - 1) + 127
    byte = np.clip(np.where(amax > 0, byte, 1), 1, 254)
    scaled = (w * np.exp2(127.0 - byte)[:, None, :]).reshape(k, n).astype(np.float32)
    by_word = np.ascontiguousarray(scaled.reshape(k // 512, 128, 4, n).transpose(0, 1, 3, 2))
    if fmt == "e4m3":
        words = by_word.astype(ml_dtypes.float8_e4m3fn).view(np.uint8)
    else:
        c = by_word.astype(ml_dtypes.float4_e2m1fn).view(np.uint8) & 0xF
        words = (c[..., 0::2] | (c[..., 1::2] << 4)).reshape(k // 512, 128, 2 * n)
    return np.ascontiguousarray(words), np.ascontiguousarray(byte.astype(np.uint8).reshape(k // 512, 16, n))


def unpack_weight(words, scales, fmt):
    g, _, n = scales.shape
    words = np.ascontiguousarray(words).reshape(g, 128, n, -1)
    if fmt == "e4m3":
        vals = words.view(ml_dtypes.float8_e4m3fn).astype(np.float64)
    else:
        nib = np.empty((g, 128, n, 4), np.uint8)
        nib[..., 0::2] = words & 0xF
        nib[..., 1::2] = words >> 4
        vals = E2M1[nib]
    vals = vals * np.repeat(np.exp2(scales.astype(np.float64) - 127.0), 8, axis=1)[..., None]
    return vals.transpose(0, 1, 3, 2).reshape(g * 512, n)


def gelu(v):
    return 0.5 * v * (1.0 + np.tanh(np.sqrt(2.0 / np.pi) * (v + 0.044715 * v**3)))


def striped8(idx):
    return np.concatenate([v.reshape(-1, 16).T for v in idx]).astype(np.uint16)


def unstriped8(offs):
    return np.stack([offs[16 * g:16 * g + 16].T.reshape(-1) for g in range(8)]).astype(np.int64)


def heads(h, wgt, idx8):
    r = np.arange(h.shape[0])
    return wgt[r // 4 % 128] * h[r[:, None], idx8[r % 512 // 64]]


def put_heads(h, wgs, idx8, t2):
    r = np.arange(h.shape[0])
    page = np.zeros((h.shape[0], t2))
    page[r[:, None], idx8[r % 512 // 64]] = wgs[r // 4 % 128] * h
    return page


T, S, P, T2, K, H, N = 2048, 1024, 512, 1024, 1024, 1024, 512

def setup_inputs():
    n = np.random.standard_normal
    s = mx_kscale(K)[:, None]
    u = mx_kscale(H)[:, None]
    d = {}
    d["tab_words"], d["tab_scales"] = pack_weight(n((K, T)) * s, "e4m3")
    d["offs"] = striped(np.random.permutation(T)[:S])
    d["w1"] = (n((K, H)) / K ** 0.5 / s * u.T).astype(np.float32)
    d["w2_words"], d["w2_scales"] = pack_weight(n((K, H)) / K ** 0.5 / s * u.T, "e2m1")
    d["offs2"] = striped8(np.stack([np.random.permutation(S)[:P] for _ in range(8)]))
    d["wgt"] = np.repeat(np.random.uniform(0.5, 2.0, (8, P)), 16, axis=0).astype(np.float32)
    d["base"] = (0.8 * n(H) * u[:, 0]).astype(np.float32)
    d["w3"] = (n((H, N)) / H ** 0.5 / u).astype(np.float32)
    d["lim"] = (0.4 + 1.2 * n((N, P))).astype(np.float32)
    d["offs3"] = striped8(np.stack([np.random.permutation(T2)[:P] for _ in range(8)]))
    d["wgo"] = np.repeat(np.random.uniform(0.5, 2.0, (8, P)), 16, axis=0).astype(np.float32)
    return d

def reference(tab_words, tab_scales, offs, w1, w2_words, w2_scales, offs2, wgt, base, w3, lim, offs3, wgo):
    v = unpack_weight(tab_words, tab_scales, "e4m3")[:, unstriped(offs)]
    w2 = unpack_weight(w2_words, w2_scales, "e2m1")
    h1 = mxq(f64(w1), 0, "e4m3").T @ v
    h2 = w2.T @ v
    h = np.maximum(h1, h2)
    x = heads(h, f64(wgt), unstriped8(offs2))
    dev = x - f64(base)[:, None]
    y = mxq(f64(w3), 0, "e4m3").T @ mxq(dev, 0, "e4m3")
    y = np.minimum(y, f64(lim))
    return put_heads(y, f64(wgo), unstriped8(offs3), T2)

@@ -1,0 +1,256 @@
+from contextlib import ExitStack
+
+import concourse.mybir as mybir
+
+F32 = mybir.dt.float32
+BF16 = mybir.dt.bfloat16
+I32 = mybir.dt.int32
+U32 = mybir.dt.uint32
+U16 = mybir.dt.uint16
+U8 = mybir.dt.uint8
+FP8X4 = mybir.dt.float8_e4m3fn_x4
+FP4X4 = mybir.dt.float4_e2m1fn_x4
+ALU = mybir.AluOpType
+ACT = mybir.ActivationFunctionType
+
+T, S, M, T2, K, H, N = 2048, 1024, 512, 1024, 1024, 1024, 512
+FLOPS = 2 * (2 * K * H * S + H * N * M)
+
+P = 128
+PACK = 4
+PASS = P * PACK
+BANK = 512
+
+
+def tile_list_cork_stopper_bins_kernel(
+    tc, tab_words, tab_scales, offs, w1, w2_words, w2_scales, offs2, wgt, base, w3, lim, offs3, wgo, out
+):
+    nc = tc.nc
+    with ExitStack() as ctx:
+        lists = ctx.enter_context(tc.tile_pool(name="lists", bufs=1))
+        keep = ctx.enter_context(tc.tile_pool(name="keep", bufs=1))
+        ring = ctx.enter_context(tc.tile_pool(name="ring", bufs=2))
+        psum = ctx.enter_context(tc.psum_pool(name="psum", bufs=8))
+
+        def kept(shape, dtype, name):
+            return keep.tile(shape, dtype, name=name, align_bytes=64)
+
+        offs_t = lists.tile([P, S // 16], U16, name="offs_t")
+        offs2_t = lists.tile([P, M // 16], U16, name="offs2_t")
+        offs3_t = lists.tile([P, M // 16], U16, name="offs3_t")
+
+        tab_sc = kept([P, T], U8, "tab_sc")
+        w2_sc_raw = kept([P, 2 * H], U8, "w2_sc_raw")
+        v_sc_low = kept([P, S], U8, "v_sc_low")
+        for t in (tab_sc, w2_sc_raw, v_sc_low):
+            nc.gpsimd.memset(t[:].bitcast(I32), 0)
+
+        def load_rows(src, rows, cols, parts=1):
+            raws = []
+            width = PASS // parts
+            for part in range(parts):
+                raw = ring.tile([P, PACK, width], F32, name="raw", bufs=3)
+                c0 = cols * PASS + part * width
+                nc.sync.dma_start(
+                    out=raw[:],
+                    in_=src[rows * PASS : (rows + 1) * PASS, c0 : c0 + width].rearrange("(p j) c -> p j c", j=PACK),
+                )
+                raws.append(raw)
+            return raws
+
+        def load_table(a):
+            words = kept([P, T], U32, "tab_w%d" % a)
+            nc.sync.dma_start(
+                out=words[:].bitcast(I32), in_=tab_words[a].rearrange("p t i -> p (t i)").bitcast(I32)
+            )
+            return words
+
+        nc.sync.dma_start(offs_t[:], offs)
+        w2_raw = kept([P, 2, H // 2], I32, "w2_raw")
+        nc.sync.dma_start(out=w2_raw[:], in_=w2_words.bitcast(I32).rearrange("a p c -> p a c"))
+        for q in range(4):
+            nc.sync.dma_start(
+                out=tab_sc[32 * q : 32 * q + 8, :].bitcast(I32), in_=tab_scales[:, 4 * q : 4 * q + 4, :].bitcast(I32)
+            )
+        tab_w = [load_table(0)]
+        w1_raw = {(0, 0): load_rows(w1, 0, 0)}
+        for q in range(4):
+            nc.sync.dma_start(
+                out=w2_sc_raw[32 * q : 32 * q + 4, :].bitcast(I32).rearrange("r (a c) -> r a c", a=2),
+                in_=w2_scales[:, 4 * q : 4 * q + 4, :].bitcast(I32).rearrange("a r c -> r a c"),
+            )
+        tab_w.append(load_table(1))
+        w1_raw[1, 0] = load_rows(w1, 1, 0, 2)
+        wgt_t = kept([P, M], F32, "wgt_t")
+        nc.sync.dma_start(out=wgt_t[:], in_=wgt)
+        nc.sync.dma_start(offs2_t[:], offs2)
+        base_t = kept([P, 2, PACK], F32, "base_t")
+        nc.sync.dma_start(out=base_t[:], in_=base.rearrange("(b p i) -> p b i", b=2, i=PACK))
+
+        pages = [kept([P, T2], F32, "page%d" % i) for i in range(PACK)]
+        for page in pages:
+            nc.vector.memset(page[:].bitcast(I32), 0)
+
+        w2_w = kept([P, 2 * H], U16, "w2_w")
+        nc.vector.tensor_copy(
+            out=w2_w[:].rearrange("p (g t m) -> p g m t", t=PACK, m=P),
+            in_=w2_raw[:].rearrange("p a c -> p (a c)").bitcast(U16).rearrange("p (g m t) -> p g m t", t=PACK, m=P),
+        )
+        v_sc = kept([P, S], U8, "v_sc")
+        nc.vector.tensor_copy(v_sc[:], tab_sc[:].indirect(offs_t[:]))
+        nc.sync.dma_start(out=v_sc_low[0 : P - 4, :].bitcast(I32), in_=v_sc[4:P, :].bitcast(I32))
+
+        def round_weights(raws, copies=(nc.scalar.copy,)):
+            grouped = ring.tile([P, PACK * PASS], BF16, name="grouped", bufs=3, align_bytes=64)
+            places = grouped[:].rearrange("p (t m j) -> p m j t", t=PACK, j=PACK)
+            share = P // len(raws)
+            for part, raw in enumerate(raws):
+                copies[part](
+                    out=places[:, part * share : (part + 1) * share],
+                    in_=raw[:].rearrange("p j (m t) -> p m j t", t=PACK),
+                )
+            return grouped
+
+        def quantize(grouped, name, parts=1):
+            codes = kept([P, PASS], U32, name + "_c")
+            scales = kept([P, PASS], U8, name + "_s")
+            width = PASS // parts
+            for part in range(parts):
+                cols = slice(part * width, (part + 1) * width)
+                nc.vector.quantize_mx(
+                    out=codes[:, cols].bitcast(FP8X4),
+                    scales=scales[:, cols],
+                    in_=grouped[:, PACK * cols.start : PACK * cols.stop],
+                )
+            return codes, scales
+
+        def gather_words(a, half):
+            words = kept([P, BANK], U32, "v_w%d%d" % (a, half))
+            cols = BANK // 16
+            nc.vector.tensor_copy(words[:], tab_w[a][:].indirect(offs_t[:, half * cols : (half + 1) * cols]))
+            return words
+
+        nbase = kept([P, 2, PACK], F32, "nbase")
+        nc.scalar.mul(nbase[:], base_t[:], -1.0)
+
+        v_w = {}
+        w1_q = {}
+        g00 = round_weights(w1_raw[0, 0])
+        v_w[0, 0] = gather_words(0, 0)
+        v_w[0, 1] = gather_words(0, 1)
+        w2_sc = kept([P, 2 * H], U8, "w2_sc")
+        nc.vector.tensor_copy(
+            out=w2_sc[:].rearrange("p (g t m) -> p g t m", t=PACK, m=P),
+            in_=w2_sc_raw[:].rearrange("p (g m t) -> p g t m", t=PACK, m=P),
+        )
+        v_w[1, 0] = gather_words(1, 0)
+        v_w[1, 1] = gather_words(1, 1)
+        w1_q[0, 0] = quantize(g00, "w1q00")
+        g10 = round_weights(w1_raw[1, 0], (nc.scalar.copy, nc.vector.tensor_copy))
+        w1_q[1, 0] = quantize(g10, "w1q10", 2)
+
+        w1_raw[0, 1] = load_rows(w1, 0, 1)
+        w1_raw[1, 1] = load_rows(w1, 1, 1)
+
+        def h_tile(b, i):
+            h2s = ring.tile([P, S], F32, name="h2s", bufs=3)
+            h = ring.tile([P, S], F32, name="h", bufs=2)
+            acc1 = []
+            for half in range(2):
+                cols = slice(half * BANK, (half + 1) * BANK)
+                acc = psum.tile([P, BANK], F32, name="acc")
+                for a in range(2):
+                    c0 = a * H + b * PASS + i * P
+                    nc.tensor.matmul_mx(
+                        out=acc[:],
+                        lhsT=w2_w[:, c0 : c0 + P].bitcast(FP4X4),
+                        lhsT_scale=w2_sc[:, c0 : c0 + P],
+                        rhs=v_w[a, half][:].bitcast(FP8X4),
+                        rhs_scale=(v_sc, v_sc_low)[a][:, cols],
+                        start=(a == 0),
+                        stop=(a == 1),
+                    )
+                nc.scalar.copy(out=h2s[:, cols], in_=acc[:])
+            for half in range(2):
+                cols = slice(half * BANK, (half + 1) * BANK)
+                acc = psum.tile([P, BANK], F32, name="acc")
+                for a in range(2):
+                    codes, scales = w1_q[a, b]
+                    nc.tensor.matmul_mx(
+                        out=acc[:],
+                        lhsT=codes[:, i * P : (i + 1) * P].bitcast(FP8X4),
+                        lhsT_scale=scales[:, i * P : (i + 1) * P],
+                        rhs=v_w[a, half][:].bitcast(FP8X4),
+                        rhs_scale=(v_sc, v_sc_low)[a][:, cols],
+                        start=(a == 0),
+                        stop=(a == 1),
+                    )
+                nc.vector.tensor_tensor(out=h[:, cols], in0=acc[:], in1=h2s[:, cols], op=ALU.max)
+            return h
+
+        def pick(h, b, i, dev_rows):
+            x = ring.tile([P, M], F32, name="x", bufs=3)
+            nc.vector.tensor_tensor(x[:], h[:].indirect(offs2_t[:]), wgt_t[:], ALU.mult)
+            nc.scalar.activation(out=dev_rows[:, i, :], in_=x[:], func=ACT.Identity, bias=nbase[:, b, i : i + 1])
+
+        def weave(engine_copy, dev_rows):
+            grouped = ring.tile([P, PACK * M], BF16, name="dev_grouped", bufs=2, align_bytes=64)
+            engine_copy(
+                out=grouped[:].rearrange("p (c u i) -> p c i u", u=4, i=PACK),
+                in_=dev_rows[:].rearrange("p i (c u) -> p c i u", u=4),
+            )
+            return grouped
+
+        dev_q = []
+        w3_q = []
+        dev_rows = [ring.tile([P, PACK, M], BF16, name="dev_rows", bufs=2) for b in range(2)]
+        hs = {}
+        hs[0] = h_tile(0, 0)
+        for n in range(8):
+            b, i = divmod(n, PACK)
+            if n == 0:
+                w1g = round_weights(w1_raw[0, 1])
+                w3_raw = [load_rows(w3, 0, 0)]
+                nc.sync.dma_start(offs3_t[:], offs3)
+            if n == 1:
+                w1_q[0, 1] = quantize(w1g, "w1q01")
+                w1g = round_weights(w1_raw[1, 1])
+                w3_raw.append(load_rows(w3, 1, 0))
+            if n == 2:
+                w1_q[1, 1] = quantize(w1g, "w1q11")
+                lim_t = ring.tile([P, PACK, M], F32, name="raw", bufs=3)
+                nc.sync.dma_start(out=lim_t[:], in_=lim.rearrange("(p i) m -> p i m", i=PACK))
+            if n == 3:
+                w3g = round_weights(w3_raw[0])
+                wgo_t = ring.tile([P, M], F32, name="raw", bufs=3)
+                nc.sync.dma_start(out=wgo_t[:], in_=wgo)
+            if n == 5:
+                devg = weave(nc.scalar.copy, dev_rows[0])
+                w3_q.append(quantize(w3g, "w3q0"))
+            if n == 6:
+                dev_q.append(quantize(devg, "devq0"))
+                w3g = round_weights(w3_raw[1])
+            if n + 1 < 8:
+                hs[n + 1] = h_tile(*divmod(n + 1, PACK))
+            pick(hs[n], b, i, dev_rows[b])
+        w3_q.append(quantize(w3g, "w3q1"))
+        devg = weave(nc.vector.tensor_copy, dev_rows[1])
+        dev_q.append(quantize(devg, "devq1"))
+
+        out_rows = out.rearrange("(p i) t -> p i t", i=PACK)
+        for i in range(PACK):
+            acc = psum.tile([P, BANK], F32, name="acc")
+            for b in range(2):
+                nc.tensor.matmul_mx(
+                    out=acc[:],
+                    lhsT=w3_q[b][0][:, i * P : (i + 1) * P].bitcast(FP8X4),
+                    lhsT_scale=w3_q[b][1][:, i * P : (i + 1) * P],
+                    rhs=dev_q[b][0][:].bitcast(FP8X4),
+                    rhs_scale=dev_q[b][1][:],
+                    start=(b == 0),
+                    stop=(b == 1),
+                )
+            z = ring.tile([P, M], F32, name="z", bufs=4)
+            nc.vector.tensor_tensor(out=z[:], in0=acc[:], in1=lim_t[:, i, :], op=ALU.min)
+            nc.vector.tensor_tensor(pages[i][:].indirect(offs3_t[:]), z[:], wgo_t[:], ALU.mult)
+            nc.sync.dma_start(out=out_rows[:, i, :], in_=pages[i][:])

@@ -30,7 +30,7 @@ def tile_list_cork_stopper_bins_kernel(
         lists = ctx.enter_context(tc.tile_pool(name="lists", bufs=1))
         keep = ctx.enter_context(tc.tile_pool(name="keep", bufs=1))
         ring = ctx.enter_context(tc.tile_pool(name="ring", bufs=2))
-        psum = ctx.enter_context(tc.psum_pool(name="psum", bufs=8))
+        psum = ctx.enter_context(tc.psum_pool(name="psum", bufs=4))
 
         def kept(shape, dtype, name):
             return keep.tile(shape, dtype, name=name, align_bytes=64)
@@ -98,7 +98,7 @@ def tile_list_cork_stopper_bins_kernel(
         )
         v_sc = kept([P, S], U8, "v_sc")
         nc.vector.tensor_copy(v_sc[:], tab_sc[:].indirect(offs_t[:]))
-        nc.sync.dma_start(out=v_sc_low[0 : P - 4, :].bitcast(I32), in_=v_sc[4:P, :].bitcast(I32))
+        nc.sync.dma_start(out=v_sc_low[0:112, :].bitcast(I32), in_=v_sc[4:116, :].bitcast(I32))
 
         def round_weights(raws, copies=(nc.scalar.copy,)):
             grouped = ring.tile([P, PACK * PASS], BF16, name="grouped", bufs=3, align_bytes=64)
@@ -111,18 +111,24 @@ def tile_list_cork_stopper_bins_kernel(
                 )
             return grouped
 
-        def quantize(grouped, name, parts=1):
-            codes = kept([P, PASS], U32, name + "_c")
-            scales = kept([P, PASS], U8, name + "_s")
-            width = PASS // parts
-            for part in range(parts):
-                cols = slice(part * width, (part + 1) * width)
-                nc.vector.quantize_mx(
-                    out=codes[:, cols].bitcast(FP8X4),
-                    scales=scales[:, cols],
-                    in_=grouped[:, PACK * cols.start : PACK * cols.stop],
-                )
+        def quantize(grouped, name, cols=slice(0, PASS), after=None):
+            width = cols.stop - cols.start
+            codes = kept([P, width], U32, after or name + "_c")
+            scales = kept([P, width], U8, name + "_s")
+            nc.vector.quantize_mx(
+                out=codes[:].bitcast(FP8X4), scales=scales[:], in_=grouped[:, PACK * cols.start : PACK * cols.stop]
+            )
             return codes, scales
+
+        def halves(grouped, name, after=(None, None)):
+            half = PASS // 2
+            return [quantize(grouped, name + "ab"[u], slice(u * half, (u + 1) * half), after[u]) for u in range(2)]
+
+        def stationary(parts, i):
+            per = PACK // len(parts)
+            codes, scales = parts[i // per]
+            cols = slice(i % per * P, (i % per + 1) * P)
+            return dict(lhsT=codes[:, cols].bitcast(FP8X4), lhsT_scale=scales[:, cols])
 
         def gather_words(a, half):
             words = kept([P, BANK], U32, "v_w%d%d" % (a, half))
@@ -145,20 +151,19 @@ def tile_list_cork_stopper_bins_kernel(
         )
         v_w[1, 0] = gather_words(1, 0)
         v_w[1, 1] = gather_words(1, 1)
-        w1_q[0, 0] = quantize(g00, "w1q00")
+        w1_q[0, 0] = [quantize(g00, "w1q00")]
         g10 = round_weights(w1_raw[1, 0], (nc.scalar.copy, nc.vector.tensor_copy))
-        w1_q[1, 0] = quantize(g10, "w1q10", 2)
+        w1_q[1, 0] = halves(g10, "w1q10")
 
         w1_raw[0, 1] = load_rows(w1, 0, 1)
         w1_raw[1, 1] = load_rows(w1, 1, 1)
 
-        def h_tile(b, i):
-            h2s = ring.tile([P, S], F32, name="h2s", bufs=3)
-            h = ring.tile([P, S], F32, name="h", bufs=2)
-            acc1 = []
+        def second_reading(n):
+            b, i = divmod(n, PACK)
+            h2s = kept([P, S], F32, "h2s%d" % n)
             for half in range(2):
                 cols = slice(half * BANK, (half + 1) * BANK)
-                acc = psum.tile([P, BANK], F32, name="acc")
+                acc = psum.tile([P, BANK], F32, name="acc2", bufs=4)
                 for a in range(2):
                     c0 = a * H + b * PASS + i * P
                     nc.tensor.matmul_mx(
@@ -171,85 +176,108 @@ def tile_list_cork_stopper_bins_kernel(
                         stop=(a == 1),
                     )
                 nc.scalar.copy(out=h2s[:, cols], in_=acc[:])
-            for half in range(2):
+            return h2s
+
+        def stronger(n, h2s):
+            b, i = divmod(n, PACK)
+            h = kept([P, S], F32, "h%d" % (n % 2 if n < 6 else n))
+            for half in (0, 1) if n == 0 else (1, 0):
                 cols = slice(half * BANK, (half + 1) * BANK)
-                acc = psum.tile([P, BANK], F32, name="acc")
+                acc = psum.tile([P, BANK], F32, name="acc1", bufs=4)
                 for a in range(2):
-                    codes, scales = w1_q[a, b]
                     nc.tensor.matmul_mx(
                         out=acc[:],
-                        lhsT=codes[:, i * P : (i + 1) * P].bitcast(FP8X4),
-                        lhsT_scale=scales[:, i * P : (i + 1) * P],
                         rhs=v_w[a, half][:].bitcast(FP8X4),
                         rhs_scale=(v_sc, v_sc_low)[a][:, cols],
                         start=(a == 0),
                         stop=(a == 1),
+                        **stationary(w1_q[a, b], i),
                     )
                 nc.vector.tensor_tensor(out=h[:, cols], in0=acc[:], in1=h2s[:, cols], op=ALU.max)
             return h
 
-        def pick(h, b, i, dev_rows):
-            x = ring.tile([P, M], F32, name="x", bufs=3)
-            nc.vector.tensor_tensor(x[:], h[:].indirect(offs2_t[:]), wgt_t[:], ALU.mult)
-            nc.scalar.activation(out=dev_rows[:, i, :], in_=x[:], func=ACT.Identity, bias=nbase[:, b, i : i + 1])
+        def pick(n, h, x):
+            b, i = divmod(n, PACK)
+            nc.vector.tensor_tensor(x, h[:].indirect(offs2_t[:]), wgt_t[:], ALU.mult)
+            if n < 6:
+                nc.gpsimd.tensor_scalar(
+                    out=dev_rows[b][:, i, :],
+                    in0=x,
+                    scalar1=1.0,
+                    scalar2=nbase[:, b, i : i + 1],
+                    op0=ALU.mult,
+                    op1=ALU.add,
+                )
+            else:
+                nc.scalar.activation(out=dev_rows[b][:, i, :], in_=x, func=ACT.Identity, bias=nbase[:, b, i : i + 1])
 
-        def weave(engine_copy, dev_rows):
+        def weave(engine_copy, rows, parts):
             grouped = ring.tile([P, PACK * M], BF16, name="dev_grouped", bufs=2, align_bytes=64)
-            engine_copy(
-                out=grouped[:].rearrange("p (c u i) -> p c i u", u=4, i=PACK),
-                in_=dev_rows[:].rearrange("p i (c u) -> p c i u", u=4),
-            )
+            share = M // 4 // parts
+            for part in range(parts):
+                runs = slice(part * share, (part + 1) * share)
+                engine_copy(
+                    out=grouped[:].rearrange("p (c u i) -> p c i u", u=4, i=PACK)[:, runs],
+                    in_=rows[:].rearrange("p i (c u) -> p c i u", u=4)[:, runs],
+                )
             return grouped
 
-        dev_q = []
-        w3_q = []
-        dev_rows = [ring.tile([P, PACK, M], BF16, name="dev_rows", bufs=2) for b in range(2)]
-        hs = {}
-        hs[0] = h_tile(0, 0)
+        dev_rows = [kept([P, PACK, M], BF16, "dev_rows%d" % b) for b in range(2)]
+        h2s = {0: second_reading(0), 1: second_reading(1)}
+        hs = {0: stronger(0, h2s[0])}
         for n in range(8):
-            b, i = divmod(n, PACK)
             if n == 0:
                 w1g = round_weights(w1_raw[0, 1])
                 w3_raw = [load_rows(w3, 0, 0)]
                 nc.sync.dma_start(offs3_t[:], offs3)
+            if n + 2 < 8:
+                h2s[n + 2] = second_reading(n + 2)
+            if n + 1 < 8:
+                hs[n + 1] = stronger(n + 1, h2s[n + 1])
             if n == 1:
-                w1_q[0, 1] = quantize(w1g, "w1q01")
-                w1g = round_weights(w1_raw[1, 1])
+                w1_q[0, 1] = [quantize(w1g, "w1q01", after="h2s1")]
                 w3_raw.append(load_rows(w3, 1, 0))
             if n == 2:
-                w1_q[1, 1] = quantize(w1g, "w1q11")
+                w1_q[1, 1] = [quantize(w1g, "w1q11", after="h2s2")]
                 lim_t = ring.tile([P, PACK, M], F32, name="raw", bufs=3)
                 nc.sync.dma_start(out=lim_t[:], in_=lim.rearrange("(p i) m -> p i m", i=PACK))
+            if n == 5:
+                w3_q = [[quantize(w3g, "w3q0", after="h2s5")]]
+                w3g = round_weights(w3_raw[1])
+            if n == 6:
+                dev_q = [[quantize(devg, "devq0", after="h2s6")]]
+            if n + 1 < 8:
+                x = h2s[n + 1][:, BANK:S]
+            else:
+                x = kept([P, M], F32, "x_last")[:]
+            pick(n, hs[n], x)
+            if n == 1:
+                w1g = round_weights(w1_raw[1, 1])
             if n == 3:
                 w3g = round_weights(w3_raw[0])
                 wgo_t = ring.tile([P, M], F32, name="raw", bufs=3)
                 nc.sync.dma_start(out=wgo_t[:], in_=wgo)
-            if n == 5:
-                devg = weave(nc.scalar.copy, dev_rows[0])
-                w3_q.append(quantize(w3g, "w3q0"))
-            if n == 6:
-                dev_q.append(quantize(devg, "devq0"))
-                w3g = round_weights(w3_raw[1])
-            if n + 1 < 8:
-                hs[n + 1] = h_tile(*divmod(n + 1, PACK))
-            pick(hs[n], b, i, dev_rows[b])
-        w3_q.append(quantize(w3g, "w3q1"))
-        devg = weave(nc.vector.tensor_copy, dev_rows[1])
-        dev_q.append(quantize(devg, "devq1"))
+            if n == 4:
+                devg = weave(nc.scalar.copy, dev_rows[0], 1)
+        w3_first = quantize(w3g, "w3q1a", slice(0, PASS // 2), after="h6")
+        devg = weave(nc.vector.tensor_copy, dev_rows[1], 2)
+        dev_q.append(halves(devg, "devq1"))
+        w3_q.append([w3_first, quantize(w3g, "w3q1b", slice(PASS // 2, PASS), after="dev_rows1")])
 
         out_rows = out.rearrange("(p i) t -> p i t", i=PACK)
         for i in range(PACK):
-            acc = psum.tile([P, BANK], F32, name="acc")
+            acc = psum.tile([P, BANK], F32, name="acc2", bufs=4)
             for b in range(2):
-                nc.tensor.matmul_mx(
-                    out=acc[:],
-                    lhsT=w3_q[b][0][:, i * P : (i + 1) * P].bitcast(FP8X4),
-                    lhsT_scale=w3_q[b][1][:, i * P : (i + 1) * P],
-                    rhs=dev_q[b][0][:].bitcast(FP8X4),
-                    rhs_scale=dev_q[b][1][:],
-                    start=(b == 0),
-                    stop=(b == 1),
-                )
+                width = M // len(dev_q[b])
+                for u, (codes, scales) in enumerate(dev_q[b]):
+                    nc.tensor.matmul_mx(
+                        out=acc[:, u * width : (u + 1) * width],
+                        rhs=codes[:].bitcast(FP8X4),
+                        rhs_scale=scales[:],
+                        start=(b == 0),
+                        stop=(b == 1 and u == 1),
+                        **stationary(w3_q[b], i),
+                    )
             z = ring.tile([P, M], F32, name="z", bufs=4)
             nc.vector.tensor_tensor(out=z[:], in0=acc[:], in1=lim_t[:, i, :], op=ALU.min)
             nc.vector.tensor_tensor(pages[i][:].indirect(offs3_t[:]), z[:], wgo_t[:], ALU.mult)

@@ -87,7 +87,7 @@ def tile_list_cork_stopper_bins_kernel(
         base_t = kept([P, 2, PACK], F32, "base_t")
         nc.sync.dma_start(out=base_t[:], in_=base.rearrange("(b p i) -> p b i", b=2, i=PACK))
 
-        pages = [kept([P, T2], F32, "page%d" % i) for i in range(PACK)]
+        pages = [kept([P, T2], F32, "page%d" % i) for i in range(2)]
         for page in pages:
             nc.vector.memset(page[:].bitcast(I32), 0)
 
@@ -100,8 +100,12 @@ def tile_list_cork_stopper_bins_kernel(
         nc.vector.tensor_copy(v_sc[:], tab_sc[:].indirect(offs_t[:]))
         nc.sync.dma_start(out=v_sc_low[0:112, :].bitcast(I32), in_=v_sc[4:116, :].bitcast(I32))
 
-        def round_weights(raws, copies=(nc.scalar.copy,)):
-            grouped = ring.tile([P, PACK * PASS], BF16, name="grouped", bufs=3, align_bytes=64)
+        for name in ("w2_raw", "tab_sc"):
+            pages.append(kept([P, T2], F32, name))
+            nc.gpsimd.memset(pages[-1][:].bitcast(I32), 0)
+
+        def round_weights(raws, name, copies=(nc.scalar.copy,)):
+            grouped = kept([P, PACK * PASS], BF16, name)
             places = grouped[:].rearrange("p (t m j) -> p m j t", t=PACK, j=PACK)
             share = P // len(raws)
             for part, raw in enumerate(raws):
@@ -109,6 +113,13 @@ def tile_list_cork_stopper_bins_kernel(
                     out=places[:, part * share : (part + 1) * share],
                     in_=raw[:].rearrange("p j (m t) -> p m j t", t=PACK),
                 )
+            return grouped
+
+        def round_two_slices(raw, first, grouped):
+            nc.scalar.copy(
+                out=grouped.rearrange("p (t m j) -> p m j t", t=2, j=PACK),
+                in_=raw[:].rearrange("p j (m t) -> p m j t", t=PACK)[:, :, :, first : first + 2],
+            )
             return grouped
 
         def quantize(grouped, name, cols=slice(0, PASS), after=None):
@@ -124,8 +135,8 @@ def tile_list_cork_stopper_bins_kernel(
             half = PASS // 2
             return [quantize(grouped, name + "ab"[u], slice(u * half, (u + 1) * half), after[u]) for u in range(2)]
 
-        def stationary(parts, i):
-            per = PACK // len(parts)
+        def stationary(parts, i, per=None):
+            per = per or PACK // len(parts)
             codes, scales = parts[i // per]
             cols = slice(i % per * P, (i % per + 1) * P)
             return dict(lhsT=codes[:, cols].bitcast(FP8X4), lhsT_scale=scales[:, cols])
@@ -141,7 +152,7 @@ def tile_list_cork_stopper_bins_kernel(
 
         v_w = {}
         w1_q = {}
-        g00 = round_weights(w1_raw[0, 0])
+        g00 = round_weights(w1_raw[0, 0], "g00")
         v_w[0, 0] = gather_words(0, 0)
         v_w[0, 1] = gather_words(0, 1)
         w2_sc = kept([P, 2 * H], U8, "w2_sc")
@@ -149,51 +160,56 @@ def tile_list_cork_stopper_bins_kernel(
             out=w2_sc[:].rearrange("p (g t m) -> p g t m", t=PACK, m=P),
             in_=w2_sc_raw[:].rearrange("p (g m t) -> p g t m", t=PACK, m=P),
         )
+        w1_q[0, 0] = [quantize(g00, "w1q00")]
         v_w[1, 0] = gather_words(1, 0)
         v_w[1, 1] = gather_words(1, 1)
-        w1_q[0, 0] = [quantize(g00, "w1q00")]
-        g10 = round_weights(w1_raw[1, 0], (nc.scalar.copy, nc.vector.tensor_copy))
+        g10 = round_weights(w1_raw[1, 0], "g10", (nc.scalar.copy, nc.vector.tensor_copy))
         w1_q[1, 0] = halves(g10, "w1q10")
 
         w1_raw[0, 1] = load_rows(w1, 0, 1)
         w1_raw[1, 1] = load_rows(w1, 1, 1)
 
-        def second_reading(n):
+        def reading_pass(which, n, half, a):
             b, i = divmod(n, PACK)
-            h2s = kept([P, S], F32, "h2s%d" % n)
-            for half in range(2):
-                cols = slice(half * BANK, (half + 1) * BANK)
-                acc = psum.tile([P, BANK], F32, name="acc2", bufs=4)
-                for a in range(2):
-                    c0 = a * H + b * PASS + i * P
-                    nc.tensor.matmul_mx(
-                        out=acc[:],
-                        lhsT=w2_w[:, c0 : c0 + P].bitcast(FP4X4),
-                        lhsT_scale=w2_sc[:, c0 : c0 + P],
-                        rhs=v_w[a, half][:].bitcast(FP8X4),
-                        rhs_scale=(v_sc, v_sc_low)[a][:, cols],
-                        start=(a == 0),
-                        stop=(a == 1),
-                    )
-                nc.scalar.copy(out=h2s[:, cols], in_=acc[:])
-            return h2s
+            if a == 0:
+                sums[which, n, half] = psum.tile([P, BANK], F32, name="acc%d" % which, bufs=4)
+            if which == 1:
+                weights = stationary(w1_q[a, b], i)
+            else:
+                c0 = a * H + b * PASS + i * P
+                weights = dict(lhsT=w2_w[:, c0 : c0 + P].bitcast(FP4X4), lhsT_scale=w2_sc[:, c0 : c0 + P])
+            nc.tensor.matmul_mx(
+                out=sums[which, n, half][:],
+                rhs=v_w[a, half][:].bitcast(FP8X4),
+                rhs_scale=(v_sc, v_sc_low)[a][:, half * BANK : (half + 1) * BANK],
+                start=(a == 0),
+                stop=(a == 1),
+                **weights,
+            )
 
-        def stronger(n, h2s):
-            b, i = divmod(n, PACK)
+        def finish_second(n, half):
+            if (2, n, half) not in sums:
+                reading_pass(2, n, half, 0)
+            reading_pass(2, n, half, 1)
+            h2s[n, half] = kept([P, BANK], F32, "h2s%d_%d" % (n, half))
+            nc.scalar.copy(out=h2s[n, half][:], in_=sums[2, n, half][:])
+
+        def second_reading(n):
+            for half in range(2):
+                finish_second(n, half)
+
+        def stronger(n):
             h = kept([P, S], F32, "h%d" % (n % 2 if n < 6 else n))
             for half in (0, 1) if n == 0 else (1, 0):
-                cols = slice(half * BANK, (half + 1) * BANK)
-                acc = psum.tile([P, BANK], F32, name="acc1", bufs=4)
-                for a in range(2):
-                    nc.tensor.matmul_mx(
-                        out=acc[:],
-                        rhs=v_w[a, half][:].bitcast(FP8X4),
-                        rhs_scale=(v_sc, v_sc_low)[a][:, cols],
-                        start=(a == 0),
-                        stop=(a == 1),
-                        **stationary(w1_q[a, b], i),
-                    )
-                nc.vector.tensor_tensor(out=h[:, cols], in0=acc[:], in1=h2s[:, cols], op=ALU.max)
+                if (1, n, half) not in sums:
+                    reading_pass(1, n, half, 0)
+                reading_pass(1, n, half, 1)
+                nc.vector.tensor_tensor(
+                    out=h[:, half * BANK : (half + 1) * BANK],
+                    in0=sums[1, n, half][:],
+                    in1=h2s[n, half][:],
+                    op=ALU.max,
+                )
             return h
 
         def pick(n, h, x):
@@ -211,74 +227,99 @@ def tile_list_cork_stopper_bins_kernel(
             else:
                 nc.scalar.activation(out=dev_rows[b][:, i, :], in_=x, func=ACT.Identity, bias=nbase[:, b, i : i + 1])
 
-        def weave(engine_copy, rows, parts):
-            grouped = ring.tile([P, PACK * M], BF16, name="dev_grouped", bufs=2, align_bytes=64)
-            share = M // 4 // parts
-            for part in range(parts):
+        def weave(copies, rows, name):
+            grouped = kept([P, PACK * M], BF16, name)
+            share = M // 4 // len(copies)
+            for part, copy in enumerate(copies):
                 runs = slice(part * share, (part + 1) * share)
-                engine_copy(
+                copy(
                     out=grouped[:].rearrange("p (c u i) -> p c i u", u=4, i=PACK)[:, runs],
                     in_=rows[:].rearrange("p i (c u) -> p c i u", u=4)[:, runs],
                 )
             return grouped
 
+        HALF = slice(0, PASS // 2)
         dev_rows = [kept([P, PACK, M], BF16, "dev_rows%d" % b) for b in range(2)]
-        h2s = {0: second_reading(0), 1: second_reading(1)}
-        hs = {0: stronger(0, h2s[0])}
+        sums = {}
+        h2s = {}
+        for which in (2, 1):
+            for n in range(2):
+                for half in range(2):
+                    reading_pass(which, n, half, 0)
+        for half in range(2):
+            for n in range(2):
+                finish_second(n, half)
+        hs = {0: stronger(0), 1: stronger(1)}
+        second_reading(2)
+        wgo_t = kept([P, M], F32, "h2s0_0")
+        nc.sync.dma_start(out=wgo_t[:], in_=wgo)
+        nc.sync.dma_start(offs3_t[:], offs3)
+        w3_raw = load_rows(w3, 0, 0)
         for n in range(8):
+            x_name = "h2s%d_1" % (n + 1)
             if n == 0:
-                w1g = round_weights(w1_raw[0, 1])
-                w3_raw = [load_rows(w3, 0, 0)]
-                nc.sync.dma_start(offs3_t[:], offs3)
-            if n + 2 < 8:
-                h2s[n + 2] = second_reading(n + 2)
-            if n + 1 < 8:
-                hs[n + 1] = stronger(n + 1, h2s[n + 1])
+                g01 = round_weights(w1_raw[0, 1], "g00")
+                w3_raw = w3_raw + load_rows(w3, 1, 0)
             if n == 1:
-                w1_q[0, 1] = [quantize(w1g, "w1q01", after="h2s1")]
-                w3_raw.append(load_rows(w3, 1, 0))
-            if n == 2:
-                w1_q[1, 1] = [quantize(w1g, "w1q11", after="h2s2")]
+                g11 = round_weights(w1_raw[1, 1], "g10")
                 lim_t = ring.tile([P, PACK, M], F32, name="raw", bufs=3)
                 nc.sync.dma_start(out=lim_t[:], in_=lim.rearrange("(p i) m -> p i m", i=PACK))
+            if n in (2, 3):
+                early = round_two_slices(w3_raw[n - 2], 0, kept([P, 2 * PASS], BF16, "w3_early%d" % (n - 2))[:])
+                w3_early = [early] if n == 2 else w3_early + [early]
+            if n + 3 < 8:
+                second_reading(n + 3)
+            if 1 < n + 1 < 8:
+                hs[n + 1] = stronger(n + 1)
+            if n == 2:
+                w1_q[0, 1] = [quantize(g01, "w1q01", after="h2s3_1")]
+                w1_q[1, 1] = [quantize(g11, "w1q11", after="h2s3_0")]
+                x_name = "g10"
             if n == 5:
-                w3_q = [[quantize(w3g, "w3q0", after="h2s5")]]
-                w3g = round_weights(w3_raw[1])
-            if n == 6:
-                dev_q = [[quantize(devg, "devq0", after="h2s6")]]
-            if n + 1 < 8:
-                x = h2s[n + 1][:, BANK:S]
-            else:
-                x = kept([P, M], F32, "x_last")[:]
-            pick(n, hs[n], x)
-            if n == 1:
-                w1g = round_weights(w1_raw[1, 1])
-            if n == 3:
-                w3g = round_weights(w3_raw[0])
-                wgo_t = ring.tile([P, M], F32, name="raw", bufs=3)
-                nc.sync.dma_start(out=wgo_t[:], in_=wgo)
+                w3_q = [[quantize(w3_early[0], "w3q0a", HALF, after="h2s6_1")]]
+                x_name = "h2s6_0"
+            pick(n, hs[n], kept([P, M], F32, x_name)[:])
             if n == 4:
-                devg = weave(nc.scalar.copy, dev_rows[0], 1)
-        w3_first = quantize(w3g, "w3q1a", slice(0, PASS // 2), after="h6")
-        devg = weave(nc.vector.tensor_copy, dev_rows[1], 2)
+                devg = weave((nc.scalar.copy,), dev_rows[0], "devg0")
+                w3_late = [round_two_slices(w3_raw[0], 2, kept([P, 2 * PASS], BF16, "dev_rows0")[:])]
+        dev_q = [[quantize(devg, "devq0", after="h6")]]
+        devg = weave((nc.vector.tensor_copy, nc.scalar.copy), dev_rows[1], "devg1")
+        w3_q.append([quantize(w3_early[1], "w3q1a", HALF, after="h2s8_1")])
         dev_q.append(halves(devg, "devq1"))
-        w3_q.append([w3_first, quantize(w3g, "w3q1b", slice(PASS // 2, PASS), after="dev_rows1")])
+        w3_late.append(round_two_slices(w3_raw[1], 2, kept([P, 2 * PASS], BF16, "dev_rows1")[:]))
+        w3_q[0].append(quantize(w3_late[0], "w3q0b", HALF, after="devg1"))
 
         out_rows = out.rearrange("(p i) t -> p i t", i=PACK)
-        for i in range(PACK):
-            acc = psum.tile([P, BANK], F32, name="acc2", bufs=4)
+
+        def grade(pair):
+            accs = [psum.tile([P, BANK], F32, name="acc2", bufs=4) for i in pair]
             for b in range(2):
                 width = M // len(dev_q[b])
                 for u, (codes, scales) in enumerate(dev_q[b]):
-                    nc.tensor.matmul_mx(
-                        out=acc[:, u * width : (u + 1) * width],
-                        rhs=codes[:].bitcast(FP8X4),
-                        rhs_scale=scales[:],
-                        start=(b == 0),
-                        stop=(b == 1 and u == 1),
-                        **stationary(w3_q[b], i),
-                    )
-            z = ring.tile([P, M], F32, name="z", bufs=4)
-            nc.vector.tensor_tensor(out=z[:], in0=acc[:], in1=lim_t[:, i, :], op=ALU.min)
+                    for i, acc in zip(pair, accs):
+                        nc.tensor.matmul_mx(
+                            out=acc[:, u * width : (u + 1) * width],
+                            rhs=codes[:].bitcast(FP8X4),
+                            rhs_scale=scales[:],
+                            start=(b == 0),
+                            stop=(b == 1 and u == 1),
+                            **stationary(w3_q[b], i, 2),
+                        )
+            held = []
+            for i, acc in zip(pair, accs):
+                z = kept([P, M], F32, "z%d" % i)
+                nc.vector.tensor_tensor(out=z[:], in0=acc[:], in1=lim_t[:, i, :], op=ALU.min)
+                held.append(z)
+            return held
+
+        def place(i, z):
             nc.vector.tensor_tensor(pages[i][:].indirect(offs3_t[:]), z[:], wgo_t[:], ALU.mult)
             nc.sync.dma_start(out=out_rows[:, i, :], in_=pages[i][:])
+
+        z0, z1 = grade((0, 1))
+        w3_q[1].append(quantize(w3_late[1], "w3q1b", HALF))
+        place(0, z0)
+        place(1, z1)
+        z2, z3 = grade((2, 3))
+        place(2, z2)
+        place(3, z3)

from contextlib import ExitStack

import concourse.mybir as mybir

F32 = mybir.dt.float32
BF16 = mybir.dt.bfloat16
I32 = mybir.dt.int32
U32 = mybir.dt.uint32
U16 = mybir.dt.uint16
U8 = mybir.dt.uint8
FP8X4 = mybir.dt.float8_e4m3fn_x4
FP4X4 = mybir.dt.float4_e2m1fn_x4
ALU = mybir.AluOpType
ACT = mybir.ActivationFunctionType

T, S, M, T2, K, H, N = 2048, 1024, 512, 1024, 1024, 1024, 512
FLOPS = 2 * (2 * K * H * S + H * N * M)

P = 128
PACK = 4
PASS = P * PACK
BANK = 512


def tile_list_cork_stopper_bins_kernel(
    tc, tab_words, tab_scales, offs, w1, w2_words, w2_scales, offs2, wgt, base, w3, lim, offs3, wgo, out
):
    nc = tc.nc
    with ExitStack() as ctx:
        lists = ctx.enter_context(tc.tile_pool(name="lists", bufs=1))
        keep = ctx.enter_context(tc.tile_pool(name="keep", bufs=1))
        ring = ctx.enter_context(tc.tile_pool(name="ring", bufs=2))
        psum = ctx.enter_context(tc.psum_pool(name="psum", bufs=4))

        def kept(shape, dtype, name):
            return keep.tile(shape, dtype, name=name, align_bytes=64)

        offs_t = lists.tile([P, S // 16], U16, name="offs_t")
        offs2_t = lists.tile([P, M // 16], U16, name="offs2_t")
        offs3_t = lists.tile([P, M // 16], U16, name="offs3_t")

        tab_sc = kept([P, T], U8, "tab_sc")
        w2_sc_raw = kept([P, 2 * H], U8, "w2_sc_raw")
        v_sc_low = kept([P, S], U8, "v_sc_low")
        for t in (tab_sc, w2_sc_raw, v_sc_low):
            nc.gpsimd.memset(t[:].bitcast(I32), 0)

        def load_rows(src, rows, cols, parts=1):
            raws = []
            width = PASS // parts
            for part in range(parts):
                raw = ring.tile([P, PACK, width], F32, name="raw", bufs=3)
                c0 = cols * PASS + part * width
                nc.sync.dma_start(
                    out=raw[:],
                    in_=src[rows * PASS : (rows + 1) * PASS, c0 : c0 + width].rearrange("(p j) c -> p j c", j=PACK),
                )
                raws.append(raw)
            return raws

        def load_table(a):
            words = kept([P, T], U32, "tab_w%d" % a)
            nc.sync.dma_start(
                out=words[:].bitcast(I32), in_=tab_words[a].rearrange("p t i -> p (t i)").bitcast(I32)
            )
            return words

        nc.sync.dma_start(offs_t[:], offs)
        w2_raw = kept([P, 2, H // 2], I32, "w2_raw")
        nc.sync.dma_start(out=w2_raw[:], in_=w2_words.bitcast(I32).rearrange("a p c -> p a c"))
        for q in range(4):
            nc.sync.dma_start(
                out=tab_sc[32 * q : 32 * q + 8, :].bitcast(I32), in_=tab_scales[:, 4 * q : 4 * q + 4, :].bitcast(I32)
            )
        tab_w = [load_table(0)]
        w1_raw = {(0, 0): load_rows(w1, 0, 0)}
        for q in range(4):
            nc.sync.dma_start(
                out=w2_sc_raw[32 * q : 32 * q + 4, :].bitcast(I32).rearrange("r (a c) -> r a c", a=2),
                in_=w2_scales[:, 4 * q : 4 * q + 4, :].bitcast(I32).rearrange("a r c -> r a c"),
            )
        tab_w.append(load_table(1))
        w1_raw[1, 0] = load_rows(w1, 1, 0, 2)
        wgt_t = kept([P, M], F32, "wgt_t")
        nc.sync.dma_start(out=wgt_t[:], in_=wgt)
        nc.sync.dma_start(offs2_t[:], offs2)
        base_t = kept([P, 2, PACK], F32, "base_t")
        nc.sync.dma_start(out=base_t[:], in_=base.rearrange("(b p i) -> p b i", b=2, i=PACK))

        pages = [kept([P, T2], F32, "page%d" % i) for i in range(2)]
        for page in pages:
            nc.vector.memset(page[:].bitcast(I32), 0)

        w2_w = kept([P, 2 * H], U16, "w2_w")
        nc.vector.tensor_copy(
            out=w2_w[:].rearrange("p (g t m) -> p g m t", t=PACK, m=P),
            in_=w2_raw[:].rearrange("p a c -> p (a c)").bitcast(U16).rearrange("p (g m t) -> p g m t", t=PACK, m=P),
        )
        v_sc = kept([P, S], U8, "v_sc")
        nc.vector.tensor_copy(v_sc[:], tab_sc[:].indirect(offs_t[:]))
        nc.sync.dma_start(out=v_sc_low[0:112, :].bitcast(I32), in_=v_sc[4:116, :].bitcast(I32))

        for name in ("w2_raw", "tab_sc"):
            pages.append(kept([P, T2], F32, name))
            nc.gpsimd.memset(pages[-1][:].bitcast(I32), 0)

        def round_weights(raws, name, copies=(nc.scalar.copy,)):
            grouped = kept([P, PACK * PASS], BF16, name)
            places = grouped[:].rearrange("p (t m j) -> p m j t", t=PACK, j=PACK)
            share = P // len(raws)
            for part, raw in enumerate(raws):
                copies[part](
                    out=places[:, part * share : (part + 1) * share],
                    in_=raw[:].rearrange("p j (m t) -> p m j t", t=PACK),
                )
            return grouped

        def round_two_slices(raw, first, grouped):
            nc.scalar.copy(
                out=grouped.rearrange("p (t m j) -> p m j t", t=2, j=PACK),
                in_=raw[:].rearrange("p j (m t) -> p m j t", t=PACK)[:, :, :, first : first + 2],
            )
            return grouped

        def quantize(grouped, name, cols=slice(0, PASS), after=None):
            width = cols.stop - cols.start
            codes = kept([P, width], U32, after or name + "_c")
            scales = kept([P, width], U8, name + "_s")
            nc.vector.quantize_mx(
                out=codes[:].bitcast(FP8X4), scales=scales[:], in_=grouped[:, PACK * cols.start : PACK * cols.stop]
            )
            return codes, scales

        def halves(grouped, name, after=(None, None)):
            half = PASS // 2
            return [quantize(grouped, name + "ab"[u], slice(u * half, (u + 1) * half), after[u]) for u in range(2)]

        def stationary(parts, i, per=None):
            per = per or PACK // len(parts)
            codes, scales = parts[i // per]
            cols = slice(i % per * P, (i % per + 1) * P)
            return dict(lhsT=codes[:, cols].bitcast(FP8X4), lhsT_scale=scales[:, cols])

        def gather_words(a, half):
            words = kept([P, BANK], U32, "v_w%d%d" % (a, half))
            cols = BANK // 16
            nc.vector.tensor_copy(words[:], tab_w[a][:].indirect(offs_t[:, half * cols : (half + 1) * cols]))
            return words

        nbase = kept([P, 2, PACK], F32, "nbase")
        nc.scalar.mul(nbase[:], base_t[:], -1.0)

        v_w = {}
        w1_q = {}
        g00 = round_weights(w1_raw[0, 0], "g00")
        v_w[0, 0] = gather_words(0, 0)
        v_w[0, 1] = gather_words(0, 1)
        w2_sc = kept([P, 2 * H], U8, "w2_sc")
        nc.vector.tensor_copy(
            out=w2_sc[:].rearrange("p (g t m) -> p g t m", t=PACK, m=P),
            in_=w2_sc_raw[:].rearrange("p (g m t) -> p g t m", t=PACK, m=P),
        )
        w1_q[0, 0] = [quantize(g00, "w1q00")]
        v_w[1, 0] = gather_words(1, 0)
        v_w[1, 1] = gather_words(1, 1)
        g10 = round_weights(w1_raw[1, 0], "g10", (nc.scalar.copy, nc.vector.tensor_copy))
        w1_q[1, 0] = halves(g10, "w1q10")

        w1_raw[0, 1] = load_rows(w1, 0, 1)
        w1_raw[1, 1] = load_rows(w1, 1, 1)

        def reading_pass(which, n, half, a):
            b, i = divmod(n, PACK)
            if a == 0:
                sums[which, n, half] = psum.tile([P, BANK], F32, name="acc%d" % which, bufs=4)
            if which == 1:
                weights = stationary(w1_q[a, b], i)
            else:
                c0 = a * H + b * PASS + i * P
                weights = dict(lhsT=w2_w[:, c0 : c0 + P].bitcast(FP4X4), lhsT_scale=w2_sc[:, c0 : c0 + P])
            nc.tensor.matmul_mx(
                out=sums[which, n, half][:],
                rhs=v_w[a, half][:].bitcast(FP8X4),
                rhs_scale=(v_sc, v_sc_low)[a][:, half * BANK : (half + 1) * BANK],
                start=(a == 0),
                stop=(a == 1),
                **weights,
            )

        def finish_second(n, half):
            if (2, n, half) not in sums:
                reading_pass(2, n, half, 0)
            reading_pass(2, n, half, 1)
            h2s[n, half] = kept([P, BANK], F32, "h2s%d_%d" % (n, half))
            nc.scalar.copy(out=h2s[n, half][:], in_=sums[2, n, half][:])

        def second_reading(n):
            for half in range(2):
                finish_second(n, half)

        def stronger(n):
            h = kept([P, S], F32, "h%d" % (n % 2 if n < 6 else n))
            for half in (0, 1) if n == 0 else (1, 0):
                if (1, n, half) not in sums:
                    reading_pass(1, n, half, 0)
                reading_pass(1, n, half, 1)
                nc.vector.tensor_tensor(
                    out=h[:, half * BANK : (half + 1) * BANK],
                    in0=sums[1, n, half][:],
                    in1=h2s[n, half][:],
                    op=ALU.max,
                )
            return h

        def pick(n, h, x):
            b, i = divmod(n, PACK)
            nc.vector.tensor_tensor(x, h[:].indirect(offs2_t[:]), wgt_t[:], ALU.mult)
            if n < 6:
                nc.gpsimd.tensor_scalar(
                    out=dev_rows[b][:, i, :],
                    in0=x,
                    scalar1=1.0,
                    scalar2=nbase[:, b, i : i + 1],
                    op0=ALU.mult,
                    op1=ALU.add,
                )
            else:
                nc.scalar.activation(out=dev_rows[b][:, i, :], in_=x, func=ACT.Identity, bias=nbase[:, b, i : i + 1])

        def weave(copies, rows, name):
            grouped = kept([P, PACK * M], BF16, name)
            share = M // 4 // len(copies)
            for part, copy in enumerate(copies):
                runs = slice(part * share, (part + 1) * share)
                copy(
                    out=grouped[:].rearrange("p (c u i) -> p c i u", u=4, i=PACK)[:, runs],
                    in_=rows[:].rearrange("p i (c u) -> p c i u", u=4)[:, runs],
                )
            return grouped

        HALF = slice(0, PASS // 2)
        dev_rows = [kept([P, PACK, M], BF16, "dev_rows%d" % b) for b in range(2)]
        sums = {}
        h2s = {}
        for which in (2, 1):
            for n in range(2):
                for half in range(2):
                    reading_pass(which, n, half, 0)
        for half in range(2):
            for n in range(2):
                finish_second(n, half)
        hs = {0: stronger(0), 1: stronger(1)}
        second_reading(2)
        wgo_t = kept([P, M], F32, "h2s0_0")
        nc.sync.dma_start(out=wgo_t[:], in_=wgo)
        nc.sync.dma_start(offs3_t[:], offs3)
        w3_raw = load_rows(w3, 0, 0)
        for n in range(8):
            x_name = "h2s%d_1" % (n + 1)
            if n == 0:
                g01 = round_weights(w1_raw[0, 1], "g00")
                w3_raw = w3_raw + load_rows(w3, 1, 0)
            if n == 1:
                g11 = round_weights(w1_raw[1, 1], "g10")
                lim_t = ring.tile([P, PACK, M], F32, name="raw", bufs=3)
                nc.sync.dma_start(out=lim_t[:], in_=lim.rearrange("(p i) m -> p i m", i=PACK))
            if n in (2, 3):
                early = round_two_slices(w3_raw[n - 2], 0, kept([P, 2 * PASS], BF16, "w3_early%d" % (n - 2))[:])
                w3_early = [early] if n == 2 else w3_early + [early]
            if n + 3 < 8:
                second_reading(n + 3)
            if 1 < n + 1 < 8:
                hs[n + 1] = stronger(n + 1)
            if n == 2:
                w1_q[0, 1] = [quantize(g01, "w1q01", after="h2s3_1")]
                w1_q[1, 1] = [quantize(g11, "w1q11", after="h2s3_0")]
                x_name = "g10"
            if n == 5:
                w3_q = [[quantize(w3_early[0], "w3q0a", HALF, after="h2s6_1")]]
                x_name = "h2s6_0"
            pick(n, hs[n], kept([P, M], F32, x_name)[:])
            if n == 4:
                devg = weave((nc.scalar.copy,), dev_rows[0], "devg0")
                w3_late = [round_two_slices(w3_raw[0], 2, kept([P, 2 * PASS], BF16, "dev_rows0")[:])]
        dev_q = [[quantize(devg, "devq0", after="h6")]]
        devg = weave((nc.vector.tensor_copy, nc.scalar.copy), dev_rows[1], "devg1")
        w3_q.append([quantize(w3_early[1], "w3q1a", HALF, after="h2s8_1")])
        dev_q.append(halves(devg, "devq1"))
        w3_late.append(round_two_slices(w3_raw[1], 2, kept([P, 2 * PASS], BF16, "dev_rows1")[:]))
        w3_q[0].append(quantize(w3_late[0], "w3q0b", HALF, after="devg1"))

        out_rows = out.rearrange("(p i) t -> p i t", i=PACK)

        def grade(pair):
            accs = [psum.tile([P, BANK], F32, name="acc2", bufs=4) for i in pair]
            for b in range(2):
                width = M // len(dev_q[b])
                for u, (codes, scales) in enumerate(dev_q[b]):
                    for i, acc in zip(pair, accs):
                        nc.tensor.matmul_mx(
                            out=acc[:, u * width : (u + 1) * width],
                            rhs=codes[:].bitcast(FP8X4),
                            rhs_scale=scales[:],
                            start=(b == 0),
                            stop=(b == 1 and u == 1),
                            **stationary(w3_q[b], i, 2),
                        )
            held = []
            for i, acc in zip(pair, accs):
                z = kept([P, M], F32, "z%d" % i)
                nc.vector.tensor_tensor(out=z[:], in0=acc[:], in1=lim_t[:, i, :], op=ALU.min)
                held.append(z)
            return held

        def place(i, z):
            nc.vector.tensor_tensor(pages[i][:].indirect(offs3_t[:]), z[:], wgo_t[:], ALU.mult)
            nc.sync.dma_start(out=out_rows[:, i, :], in_=pages[i][:])

        z0, z1 = grade((0, 1))
        w3_q[1].append(quantize(w3_late[1], "w3q1b", HALF))
        place(0, z0)
        place(1, z1)
        z2, z3 = grade((2, 3))
        place(2, z2)
        place(3, z3)
